import numpy as np, ml_dtypes
CORES = [16,17,18,19,150,151]
N = 6
TK = 64
def setup_inputs(rng):
    return {"x": rng.standard_normal((N, 128, N * TK), dtype=np.float32).astype(ml_dtypes.bfloat16), "t": rng.standard_normal((N, 128, N * TK), dtype=np.float32).astype(ml_dtypes.bfloat16), "f1": (rng.standard_normal((N, 128, 128), dtype=np.float32) / 11).astype(ml_dtypes.bfloat16), "f2": (rng.standard_normal((N, 128, 128), dtype=np.float32) / 11).astype(ml_dtypes.bfloat16)}
def setup_inputs_big(rng):
    d = setup_inputs(rng)
    for k in ("x", "t", "f1", "f2"): d[k] = (d[k].astype(np.float32) * 1024.0).astype(d[k].dtype)
    return d
def setup_inputs_small(rng):
    d = setup_inputs(rng)
    for k in ("x", "t", "f1", "f2"): d[k] = (d[k].astype(np.float32) * (1 / 1024.0)).astype(d[k].dtype)
    return d
def reference(x, t, f1, f2):
    X, T, F1, F2 = x.astype(np.float64), t.astype(np.float64), f1.astype(np.float64), f2.astype(np.float64)
    y = np.zeros((N, 128, N * TK))
    for j in range(N):
        u = (F1[j].T @ X[j]) * T[j]
        for r in range(N):
            y[r][:, TK * j:TK * j + TK] = F2[r].T @ u[:, TK * r:TK * r + TK]
    return {"y": y.astype(ml_dtypes.bfloat16)}

@@ -1,0 +1,146 @@
+from concourse.bass import DstId, RemoteDMATransfer
+from concourse.mybir import AluOpType
+
+SCRATCH = {
+    "f1s": ("sbuf", [128, 128], "bfloat16"),
+    "f2s": ("sbuf", [128, 128], "bfloat16"),
+    "xs": ("sbuf", [128, 384], "bfloat16"),
+    "ts": ("sbuf", [128, 384], "bfloat16"),
+    "u": ("sbuf", [128, 384], "bfloat16"),
+    "land": ("sbuf", [128, 384], "bfloat16"),
+    "ys": ("sbuf", [128, 384], "bfloat16"),
+    "p1far": ("psum", [128, 512], "float32"),
+    "p1home": ("psum", [128, 512], "float32"),
+    "p2far": ("psum", [128, 512], "float32"),
+    "p2home": ("psum", [128, 512], "float32"),
+}
+SEMAPHORES = ["ld_mm", "ld_t", "ld_f2", "mm1_far", "mm1_home", "u_far", "u_home", "arr_far", "arr_near", "sent",
+              "mm2_far", "mm2_home", "cp_far", "cp_home", "st_far", "st_home"]
+
+FAR_ENGINES = 2
+NEAR_ENGINES = 2
+
+
+def _same_chip(topo, a, b):
+    return topo.host(a) == topo.host(b) and topo.chip(a) == topo.chip(b)
+
+
+def _bits(mask):
+    return [1 << i for i in range(mask.bit_length()) if (mask >> i) & 1]
+
+
+def _runs(blocks, w):
+    out = []
+    for b in blocks:
+        if out and out[-1][1] == b * w:
+            out[-1][1] = (b + 1) * w
+        else:
+            out.append([b * w, (b + 1) * w])
+    return [(lo, hi) for lo, hi in out]
+
+
+def _plan(topo, cores, src):
+    far = [d for d in cores if not _same_chip(topo, src, d)]
+    near = [d for d in cores if d != src and _same_chip(topo, src, d)]
+    off = None
+    for d in far:
+        off = topo.mask(src, d) if off is None else off & topo.mask(src, d)
+    off = _bits(off or 0)
+    pool = off[0::2] + off[1::2]
+    far_w = []
+    for d in far:
+        use, pool = pool[:FAR_ENGINES], pool[FAR_ENGINES:]
+        far_w.append((d, sum(use), len(use)))
+    on = None
+    for d in near:
+        on = topo.mask(src, d) if on is None else on & topo.mask(src, d)
+    on = _bits(on or 0)
+    pool = [b for b in on if b not in off] + [b for b in pool if b in on]
+    near_w = []
+    for d in near:
+        use, pool = pool[:NEAR_ENGINES], pool[NEAR_ENGINES:]
+        near_w.append((d, sum(use), len(use)))
+    return far_w, near_w
+
+
+def rank_program(g, core, T, topo):
+    rank = T.rank_of(core)
+    if rank is None:
+        return
+    cores = list(T.cores)
+    n = len(cores)
+    w = T.x.shape[1] // n
+    S = T.sem
+    far = [j for j in range(n) if not _same_chip(topo, core, cores[j])]
+    home = [j for j in range(n) if _same_chip(topo, core, cores[j])]
+    near = [j for j in home if j != rank]
+    far_runs, home_runs, near_runs = _runs(far, w), _runs(home, w), _runs(near, w)
+    own = (rank * w, (rank + 1) * w)
+
+    g.sync.dma_start(T.f1s[:], T.f1[:]).then_inc(S.ld_mm, 16)
+    g.scalar.dma_start(T.xs[:], T.x[:]).then_inc(S.ld_mm, 16)
+    g.sync.dma_start(T.ts[:], T.t[:]).then_inc(S.ld_t, 16)
+    g.scalar.wait_ge(S.ld_t, 16)
+    g.scalar.dma_start(T.f2s[:], T.f2[:]).then_inc(S.ld_f2, 16)
+
+    g.tensor.wait_ge(S.ld_mm, 32)
+    for lo, hi in far_runs:
+        g.tensor.matmul(T.p1far[:, lo:hi], T.f1s[:], T.xs[:, lo:hi], True, True).then_inc(S.mm1_far, 1)
+    for lo, hi in home_runs:
+        g.tensor.matmul(T.p1home[:, lo:hi], T.f1s[:], T.xs[:, lo:hi], True, True).then_inc(S.mm1_home, 1)
+    g.vector.wait_ge(S.ld_t, 16)
+    g.vector.wait_ge(S.mm1_far, len(far_runs))
+    for lo, hi in far_runs:
+        g.vector.tensor_tensor(T.u[:, lo:hi], T.p1far[:, lo:hi], T.ts[:, lo:hi], AluOpType.mult).then_inc(S.u_far, 1)
+    g.vector.wait_ge(S.mm1_home, len(home_runs))
+    for lo, hi in home_runs:
+        g.vector.tensor_tensor(T.u[:, lo:hi], T.p1home[:, lo:hi], T.ts[:, lo:hi], AluOpType.mult).then_inc(S.u_home, 1)
+
+    far_w, near_w = _plan(topo, cores, core)
+    sent = 0
+    for writes, ready, cnt, arr in ((far_w, S.u_far, len(far_runs), S.arr_far),
+                                    (near_w, S.u_home, len(home_runs), S.arr_near)):
+        if not writes:
+            continue
+        g.wait_ge(ready, cnt)
+        trs = []
+        for d, m, e in writes:
+            rid, pid = topo.addr(d, core)
+            r = T.rank_of(d)
+            trs.append(RemoteDMATransfer(dst_ids=[DstId(rid=rid, pnc=pid)], dma_engine_mask=m, remote_sem=arr,
+                                         src=T.u[:, r * w:(r + 1) * w], dst=T.land[:, own[0]:own[1]]))
+            sent += e
+        g.remote_dma_fused(trs, local_sem=S.sent)
+
+    in_far = sum(e for j in far for d, m, e in _plan(topo, cores, cores[j])[0] if d == core)
+    in_near = sum(e for j in near for d, m, e in _plan(topo, cores, cores[j])[1] if d == core)
+
+    g.tensor.wait_ge(S.ld_f2, 16)
+    g.tensor.wait_ge(S.u_home, len(home_runs))
+    g.tensor.matmul(T.p2home[:, own[0]:own[1]], T.f2s[:], T.u[:, own[0]:own[1]], True, True).then_inc(S.mm2_home, 1)
+    if near:
+        g.tensor.wait_ge(S.arr_near, in_near)
+    for lo, hi in near_runs:
+        g.tensor.matmul(T.p2home[:, lo:hi], T.f2s[:], T.land[:, lo:hi], True, True).then_inc(S.mm2_home, 1)
+    if far:
+        g.tensor.wait_ge(S.arr_far, in_far)
+    for lo, hi in far_runs:
+        g.tensor.matmul(T.p2far[:, lo:hi], T.f2s[:], T.land[:, lo:hi], True, True).then_inc(S.mm2_far, 1)
+
+    g.vector.wait_ge(S.mm2_home, 1 + len(near_runs))
+    for lo, hi in home_runs:
+        g.vector.tensor_copy(T.ys[:, lo:hi], T.p2home[:, lo:hi]).then_inc(S.cp_home, 1)
+    g.vector.wait_ge(S.mm2_far, len(far_runs))
+    for lo, hi in far_runs:
+        g.vector.tensor_copy(T.ys[:, lo:hi], T.p2far[:, lo:hi]).then_inc(S.cp_far, 1)
+
+    g.sync.wait_ge(S.cp_home, len(home_runs))
+    for lo, hi in home_runs:
+        g.sync.dma_start(T.y[:, lo:hi], T.ys[:, lo:hi]).then_inc(S.st_home, 16)
+    g.scalar.wait_ge(S.cp_far, len(far_runs))
+    for lo, hi in far_runs:
+        g.scalar.dma_start(T.y[:, lo:hi], T.ys[:, lo:hi]).then_inc(S.st_far, 16)
+
+    g.wait_ge(S.sent, sent)
+    g.sync.wait_ge(S.st_home, 16 * len(home_runs))
+    g.scalar.wait_ge(S.st_far, 16 * len(far_runs))

@@ -9,13 +9,18 @@ SCRATCH = {
     "u": ("sbuf", [128, 384], "bfloat16"),
     "land": ("sbuf", [128, 384], "bfloat16"),
     "ys": ("sbuf", [128, 384], "bfloat16"),
-    "p1far": ("psum", [128, 512], "float32"),
-    "p1home": ("psum", [128, 512], "float32"),
-    "p2far": ("psum", [128, 512], "float32"),
-    "p2home": ("psum", [128, 512], "float32"),
+    "p1_0": ("psum", [128, 512], "float32"),
+    "p1_1": ("psum", [128, 512], "float32"),
+    "p1_2": ("psum", [128, 512], "float32"),
+    "p1_3": ("psum", [128, 512], "float32"),
+    "p2own": ("psum", [128, 512], "float32"),
+    "p2near": ("psum", [128, 512], "float32"),
+    "p2far_0": ("psum", [128, 512], "float32"),
+    "p2far_1": ("psum", [128, 512], "float32"),
 }
-SEMAPHORES = ["ld_mm", "ld_t", "ld_f2", "mm1_far", "mm1_home", "u_far", "u_home", "arr_far", "arr_near", "sent",
-              "mm2_far", "mm2_home", "cp_far", "cp_home", "st_far", "st_home"]
+SEMAPHORES = (["ld_f1", "ld_f2", "arr_near", "sent", "mm2_own", "mm2_near", "cp_own", "cp_near", "st_home"]
+              + ["%s_%d" % (s, k) for s in ("arr_far", "mm2_far", "cp_far", "st_far") for k in range(2)]
+              + ["%s_%d" % (s, k) for s in ("ldx", "ldt", "mm1", "u") for k in range(4)])
 
 FAR_ENGINES = 2
 NEAR_ENGINES = 2
@@ -40,27 +45,35 @@ def _runs(blocks, w):
 
 
 def _plan(topo, cores, src):
+    home = [d for d in cores if _same_chip(topo, src, d)]
     far = [d for d in cores if not _same_chip(topo, src, d)]
-    near = [d for d in cores if d != src and _same_chip(topo, src, d)]
+    near = [d for d in home if d != src]
+    rot = (home.index(src) * len(far)) // len(home)
+    far = far[rot:] + far[:rot]
     off = None
     for d in far:
         off = topo.mask(src, d) if off is None else off & topo.mask(src, d)
     off = _bits(off or 0)
-    pool = off[0::2] + off[1::2]
-    far_w = []
-    for d in far:
-        use, pool = pool[:FAR_ENGINES], pool[FAR_ENGINES:]
-        far_w.append((d, sum(use), len(use)))
+    pool = (off[0::2] + off[1::2])[:FAR_ENGINES * len(far)]
+    half = (len(far) + 1) // 2
+    waves = []
+    for dsts in (far[:half], far[half:]):
+        if not dsts:
+            continue
+        per = 1
+        while per * 2 * len(dsts) <= len(pool):
+            per *= 2
+        waves.append([(d, sum(pool[i * per:(i + 1) * per]), per) for i, d in enumerate(dsts)])
     on = None
     for d in near:
         on = topo.mask(src, d) if on is None else on & topo.mask(src, d)
     on = _bits(on or 0)
-    pool = [b for b in on if b not in off] + [b for b in pool if b in on]
+    rest = [b for b in on if b not in off] + [b for b in on if b in off and b not in pool]
     near_w = []
     for d in near:
-        use, pool = pool[:NEAR_ENGINES], pool[NEAR_ENGINES:]
+        use, rest = rest[:NEAR_ENGINES], rest[NEAR_ENGINES:]
         near_w.append((d, sum(use), len(use)))
-    return far_w, near_w
+    return waves, near_w
 
 
 def rank_program(g, core, T, topo):
@@ -74,35 +87,41 @@ def rank_program(g, core, T, topo):
     far = [j for j in range(n) if not _same_chip(topo, core, cores[j])]
     home = [j for j in range(n) if _same_chip(topo, core, cores[j])]
     near = [j for j in home if j != rank]
-    far_runs, home_runs, near_runs = _runs(far, w), _runs(home, w), _runs(near, w)
+    home_runs, near_runs = _runs(home, w), _runs(near, w)
     own = (rank * w, (rank + 1) * w)
+    waves, near_w = _plan(topo, cores, core)
 
-    g.sync.dma_start(T.f1s[:], T.f1[:]).then_inc(S.ld_mm, 16)
-    g.scalar.dma_start(T.xs[:], T.x[:]).then_inc(S.ld_mm, 16)
-    g.sync.dma_start(T.ts[:], T.t[:]).then_inc(S.ld_t, 16)
-    g.scalar.wait_ge(S.ld_t, 16)
+    far_groups = [(_runs(sorted(T.rank_of(d) for d, m, e in wv), w), wv, S["arr_far_%d" % i])
+                  for i, wv in enumerate(waves)]
+    if len(near) < len(far):
+        groups = [(near_runs, near_w, S.arr_near)] + far_groups + [([own], None, None)]
+    else:
+        groups = far_groups + [(home_runs, near_w, S.arr_near)]
+    k_own = len(groups) - 1
+
+    g.sync.dma_start(T.f1s[:], T.f1[:]).then_inc(S.ld_f1, 16)
+    for k, (runs, _w, _a) in enumerate(groups):
+        for lo, hi in runs:
+            g.scalar.dma_start(T.xs[:, lo:hi], T.x[:, lo:hi]).then_inc(S["ldx_%d" % k], 16)
+            g.sync.dma_start(T.ts[:, lo:hi], T.t[:, lo:hi]).then_inc(S["ldt_%d" % k], 16)
     g.scalar.dma_start(T.f2s[:], T.f2[:]).then_inc(S.ld_f2, 16)
 
-    g.tensor.wait_ge(S.ld_mm, 32)
-    for lo, hi in far_runs:
-        g.tensor.matmul(T.p1far[:, lo:hi], T.f1s[:], T.xs[:, lo:hi], True, True).then_inc(S.mm1_far, 1)
-    for lo, hi in home_runs:
-        g.tensor.matmul(T.p1home[:, lo:hi], T.f1s[:], T.xs[:, lo:hi], True, True).then_inc(S.mm1_home, 1)
-    g.vector.wait_ge(S.ld_t, 16)
-    g.vector.wait_ge(S.mm1_far, len(far_runs))
-    for lo, hi in far_runs:
-        g.vector.tensor_tensor(T.u[:, lo:hi], T.p1far[:, lo:hi], T.ts[:, lo:hi], AluOpType.mult).then_inc(S.u_far, 1)
-    g.vector.wait_ge(S.mm1_home, len(home_runs))
-    for lo, hi in home_runs:
-        g.vector.tensor_tensor(T.u[:, lo:hi], T.p1home[:, lo:hi], T.ts[:, lo:hi], AluOpType.mult).then_inc(S.u_home, 1)
+    g.tensor.wait_ge(S.ld_f1, 16)
+    for k, (runs, _w, _a) in enumerate(groups):
+        p = T["p1_%d" % k]
+        g.tensor.wait_ge(S["ldx_%d" % k], 16 * len(runs))
+        for lo, hi in runs:
+            g.tensor.matmul(p[:, lo:hi], T.f1s[:], T.xs[:, lo:hi], True, True).then_inc(S["mm1_%d" % k], 1)
+        g.vector.wait_ge(S["ldt_%d" % k], 16 * len(runs))
+        g.vector.wait_ge(S["mm1_%d" % k], len(runs))
+        for lo, hi in runs:
+            g.vector.tensor_tensor(T.u[:, lo:hi], p[:, lo:hi], T.ts[:, lo:hi], AluOpType.mult).then_inc(S["u_%d" % k], 1)
 
-    far_w, near_w = _plan(topo, cores, core)
     sent = 0
-    for writes, ready, cnt, arr in ((far_w, S.u_far, len(far_runs), S.arr_far),
-                                    (near_w, S.u_home, len(home_runs), S.arr_near)):
+    for k, (runs, writes, arr) in enumerate(groups):
         if not writes:
             continue
-        g.wait_ge(ready, cnt)
+        g.wait_ge(S["u_%d" % k], len(runs))
         trs = []
         for d, m, e in writes:
             rid, pid = topo.addr(d, core)
@@ -112,35 +131,46 @@ def rank_program(g, core, T, topo):
             sent += e
         g.remote_dma_fused(trs, local_sem=S.sent)
 
-    in_far = sum(e for j in far for d, m, e in _plan(topo, cores, cores[j])[0] if d == core)
     in_near = sum(e for j in near for d, m, e in _plan(topo, cores, cores[j])[1] if d == core)
+    got, cnt = [[], []], [0, 0]
+    for j in far:
+        for i, wv in enumerate(_plan(topo, cores, cores[j])[0]):
+            for d, m, e in wv:
+                if d == core:
+                    got[i].append(j)
+                    cnt[i] += e
+    pieces = [(i, lo, hi) for i in range(2) for lo, hi in _runs(got[i], w)]
 
     g.tensor.wait_ge(S.ld_f2, 16)
-    g.tensor.wait_ge(S.u_home, len(home_runs))
-    g.tensor.matmul(T.p2home[:, own[0]:own[1]], T.f2s[:], T.u[:, own[0]:own[1]], True, True).then_inc(S.mm2_home, 1)
-    if near:
-        g.tensor.wait_ge(S.arr_near, in_near)
+    g.tensor.wait_ge(S["u_%d" % k_own], len(groups[k_own][0]))
+    g.tensor.matmul(T.p2own[:, own[0]:own[1]], T.f2s[:], T.u[:, own[0]:own[1]], True, True).then_inc(S.mm2_own, 1)
+    g.tensor.wait_ge(S.arr_near, in_near)
     for lo, hi in near_runs:
-        g.tensor.matmul(T.p2home[:, lo:hi], T.f2s[:], T.land[:, lo:hi], True, True).then_inc(S.mm2_home, 1)
-    if far:
-        g.tensor.wait_ge(S.arr_far, in_far)
-    for lo, hi in far_runs:
-        g.tensor.matmul(T.p2far[:, lo:hi], T.f2s[:], T.land[:, lo:hi], True, True).then_inc(S.mm2_far, 1)
+        g.tensor.matmul(T.p2near[:, lo:hi], T.f2s[:], T.land[:, lo:hi], True, True).then_inc(S.mm2_near, 1)
+    for q, (i, lo, hi) in enumerate(pieces):
+        g.tensor.wait_ge(S["arr_far_%d" % i], cnt[i])
+        g.tensor.matmul(T["p2far_%d" % q][:, lo:hi], T.f2s[:], T.land[:, lo:hi], True, True).then_inc(S["mm2_far_%d" % q], 1)
 
-    g.vector.wait_ge(S.mm2_home, 1 + len(near_runs))
-    for lo, hi in home_runs:
-        g.vector.tensor_copy(T.ys[:, lo:hi], T.p2home[:, lo:hi]).then_inc(S.cp_home, 1)
-    g.vector.wait_ge(S.mm2_far, len(far_runs))
-    for lo, hi in far_runs:
-        g.vector.tensor_copy(T.ys[:, lo:hi], T.p2far[:, lo:hi]).then_inc(S.cp_far, 1)
+    g.vector.wait_ge(S.mm2_own, 1)
+    g.vector.tensor_copy(T.ys[:, own[0]:own[1]], T.p2own[:, own[0]:own[1]]).then_inc(S.cp_own, 1)
+    g.vector.wait_ge(S.mm2_near, len(near_runs))
+    for lo, hi in near_runs:
+        g.vector.tensor_copy(T.ys[:, lo:hi], T.p2near[:, lo:hi]).then_inc(S.cp_near, 1)
+    for q, (i, lo, hi) in enumerate(pieces):
+        g.vector.wait_ge(S["mm2_far_%d" % q], 1)
+        g.vector.tensor_copy(T.ys[:, lo:hi], T["p2far_%d" % q][:, lo:hi]).then_inc(S["cp_far_%d" % q], 1)
 
-    g.sync.wait_ge(S.cp_home, len(home_runs))
+    g.sync.wait_ge(S.cp_own, 1)
+    g.sync.wait_ge(S.cp_near, len(near_runs))
     for lo, hi in home_runs:
         g.sync.dma_start(T.y[:, lo:hi], T.ys[:, lo:hi]).then_inc(S.st_home, 16)
-    g.scalar.wait_ge(S.cp_far, len(far_runs))
-    for lo, hi in far_runs:
-        g.scalar.dma_start(T.y[:, lo:hi], T.ys[:, lo:hi]).then_inc(S.st_far, 16)
+    last = len(pieces) - 1
+    for q, (i, lo, hi) in enumerate(pieces):
+        eng = g.scalar if q == last else g.sync
+        eng.wait_ge(S["cp_far_%d" % q], 1)
+        eng.dma_start(T.y[:, lo:hi], T.ys[:, lo:hi]).then_inc(S["st_far_%d" % q], 16)
 
     g.wait_ge(S.sent, sent)
     g.sync.wait_ge(S.st_home, 16 * len(home_runs))
-    g.scalar.wait_ge(S.st_far, 16 * len(far_runs))
+    for q in range(len(pieces)):
+        (g.scalar if q == last else g.sync).wait_ge(S["st_far_%d" % q], 16)

@@ -6,24 +6,23 @@ SCRATCH = {
     "f2s": ("sbuf", [128, 128], "bfloat16"),
     "xs": ("sbuf", [128, 384], "bfloat16"),
     "ts": ("sbuf", [128, 384], "bfloat16"),
+    "tn": ("sbuf", [128, 64], "bfloat16"),
+    "tl": ("sbuf", [128, 64], "bfloat16"),
+    "uq": ("sbuf", [128, 64], "bfloat16"),
     "u": ("sbuf", [128, 384], "bfloat16"),
     "land": ("sbuf", [128, 384], "bfloat16"),
     "ys": ("sbuf", [128, 384], "bfloat16"),
-    "p1_0": ("psum", [128, 512], "float32"),
-    "p1_1": ("psum", [128, 512], "float32"),
-    "p1_2": ("psum", [128, 512], "float32"),
-    "p1_3": ("psum", [128, 512], "float32"),
-    "p2own": ("psum", [128, 512], "float32"),
-    "p2near": ("psum", [128, 512], "float32"),
-    "p2far_0": ("psum", [128, 512], "float32"),
-    "p2far_1": ("psum", [128, 512], "float32"),
 }
-SEMAPHORES = (["ld_f1", "ld_f2", "arr_near", "sent", "mm2_own", "mm2_near", "cp_own", "cp_near", "st_home"]
-              + ["%s_%d" % (s, k) for s in ("arr_far", "mm2_far", "cp_far", "st_far") for k in range(2)]
-              + ["%s_%d" % (s, k) for s in ("ldx", "ldt", "mm1", "u") for k in range(4)])
+for _k in range(8):
+    SCRATCH["b%d" % _k] = ("psum", [128, 512], "float32")
 
-FAR_ENGINES = 2
-NEAR_ENGINES = 2
+SEMAPHORES = (["ld_tn", "ld_f1", "ld_f2", "arr_t", "arr_p", "arr_near", "sent", "uq",
+               "mm2_own", "mm2_near", "mm2_p", "cp_own", "cp_near", "cp_p", "st_home"]
+              + ["%s_%d" % (s, k) for s in ("arr_far", "mm2_far", "cp_far", "st_far") for k in range(2)]
+              + ["%s_%d" % (s, k) for s in ("ldx", "ldt") for k in range(3)]
+              + ["%s_%d" % (s, k) for s in ("mm1", "u") for k in range(6)])
+
+ENG = 4
 
 
 def _same_chip(topo, a, b):
@@ -44,36 +43,44 @@ def _runs(blocks, w):
     return [(lo, hi) for lo, hi in out]
 
 
-def _plan(topo, cores, src):
+def _layout(topo, cores, src):
     home = [d for d in cores if _same_chip(topo, src, d)]
     far = [d for d in cores if not _same_chip(topo, src, d)]
-    near = [d for d in home if d != src]
-    rot = (home.index(src) * len(far)) // len(home)
+    i = home.index(src)
+    nxt = home[(i + 1) % len(home)]
+    others = [d for d in home if d != src and d != nxt]
+    rot = (i * len(far)) // len(home)
     far = far[rot:] + far[:rot]
     off = None
     for d in far:
         off = topo.mask(src, d) if off is None else off & topo.mask(src, d)
-    off = _bits(off or 0)
-    pool = (off[0::2] + off[1::2])[:FAR_ENGINES * len(far)]
-    half = (len(far) + 1) // 2
-    waves = []
-    for dsts in (far[:half], far[half:]):
-        if not dsts:
-            continue
-        per = 1
-        while per * 2 * len(dsts) <= len(pool):
-            per *= 2
-        waves.append([(d, sum(pool[i * per:(i + 1) * per]), per) for i, d in enumerate(dsts)])
     on = None
-    for d in near:
-        on = topo.mask(src, d) if on is None else on & topo.mask(src, d)
-    on = _bits(on or 0)
-    rest = [b for b in on if b not in off] + [b for b in on if b in off and b not in pool]
-    near_w = []
-    for d in near:
-        use, rest = rest[:NEAR_ENGINES], rest[NEAR_ENGINES:]
-        near_w.append((d, sum(use), len(use)))
-    return waves, near_w
+    for d in home:
+        if d != src:
+            on = topo.mask(src, d) if on is None else on & topo.mask(src, d)
+    off = _bits(off)
+    sets = [off[0::2][:ENG], off[1::2][:ENG]]
+    pset = [b for b in _bits(on) if b not in off][:ENG]
+    return home, far, nxt, others, sets, pset
+
+
+def _calls(topo, cores, src):
+    home, far, nxt, others, sets, pset = _layout(topo, cores, src)
+    calls = [[("far", d, sets[i % 2])] for i, d in enumerate(far)]
+    nearc = [("p", nxt, pset)] + [("near", d, sets[i % 2]) for i, d in enumerate(others)]
+    if others or len(calls) < 3:
+        calls.append(nearc)
+    else:
+        calls[2] = calls[2] + nearc
+    return calls
+
+
+def _far_groups(topo, cores, dst):
+    by = {}
+    for s in cores:
+        if not _same_chip(topo, s, dst):
+            by.setdefault(_layout(topo, cores, s)[1].index(dst), []).append(s)
+    return [by[k] for k in sorted(by)]
 
 
 def rank_program(g, core, T, topo):
@@ -84,93 +91,168 @@ def rank_program(g, core, T, topo):
     n = len(cores)
     w = T.x.shape[1] // n
     S = T.sem
-    far = [j for j in range(n) if not _same_chip(topo, core, cores[j])]
-    home = [j for j in range(n) if _same_chip(topo, core, cores[j])]
-    near = [j for j in home if j != rank]
-    home_runs, near_runs = _runs(home, w), _runs(near, w)
+    R = T.rank_of
+    home_c, far_c, nxt_c, others_c, sets, pset = _layout(topo, cores, core)
+    home = sorted(R(d) for d in home_c)
+    nxt = R(nxt_c)
+    others = sorted(R(d) for d in others_c)
+    prv_c = [d for d in home_c if d != core and _layout(topo, cores, d)[2] == core][0]
+    prv = R(prv_c)
+    home_runs = _runs(home, w)
     own = (rank * w, (rank + 1) * w)
-    waves, near_w = _plan(topo, cores, core)
+    calls = _calls(topo, cores, core)
 
-    far_groups = [(_runs(sorted(T.rank_of(d) for d, m, e in wv), w), wv, S["arr_far_%d" % i])
-                  for i, wv in enumerate(waves)]
-    if len(near) < len(far):
-        groups = [(near_runs, near_w, S.arr_near)] + far_groups + [([own], None, None)]
-    else:
-        groups = far_groups + [(home_runs, near_w, S.arr_near)]
-    k_own = len(groups) - 1
+    far_r = [R(d) for d in far_c]
+    chunks = [far_r[i:i + 2] for i in range(0, len(far_r), 2)]
+    H = len(chunks)
+    chunk_of = {}
+    for c, bl in enumerate(chunks):
+        for b in bl:
+            chunk_of[b] = c
+    t_home = _runs(sorted(others + [rank]), w)
+    if len(t_home) > len(home_runs):
+        t_home = home_runs
 
-    g.sync.dma_start(T.f1s[:], T.f1[:]).then_inc(S.ld_f1, 16)
-    for k, (runs, _w, _a) in enumerate(groups):
-        for lo, hi in runs:
-            g.scalar.dma_start(T.xs[:, lo:hi], T.x[:, lo:hi]).then_inc(S["ldx_%d" % k], 16)
-            g.sync.dma_start(T.ts[:, lo:hi], T.t[:, lo:hi]).then_inc(S["ldt_%d" % k], 16)
-    g.scalar.dma_start(T.f2s[:], T.f2[:]).then_inc(S.ld_f2, 16)
+    loads = [(T.tn[:], T.t[:, nxt * w:(nxt + 1) * w], S.ld_tn), (T.f1s[:], T.f1[:], S.ld_f1)]
+    nx, nt = {}, {}
+    for c, bl in enumerate(chunks):
+        rr = _runs(sorted(bl), w)
+        nx[c] = nt[c] = 16 * len(rr)
+        for lo, hi in rr:
+            loads.append((T.xs[:, lo:hi], T.x[:, lo:hi], S["ldx_%d" % c]))
+            loads.append((T.ts[:, lo:hi], T.t[:, lo:hi], S["ldt_%d" % c]))
+    nx[H], nt[H] = 16 * len(home_runs), 16 * len(t_home)
+    for lo, hi in home_runs:
+        loads.append((T.xs[:, lo:hi], T.x[:, lo:hi], S["ldx_%d" % H]))
+    for lo, hi in t_home:
+        loads.append((T.ts[:, lo:hi], T.t[:, lo:hi], S["ldt_%d" % H]))
+    loads.append((T.f2s[:], T.f2[:], S.ld_f2))
+    for i, (o, a, s) in enumerate(loads):
+        (g.sync if i % 2 == 0 else g.scalar).dma_start(o, a).then_inc(s, 16)
+
+    groups, gid = [], {}
+
+    def add(blocks, chunk, mul):
+        for lo, hi in _runs(sorted(blocks), w):
+            for b in blocks:
+                if lo <= b * w < hi:
+                    gid[b] = len(groups)
+            groups.append((lo, hi, chunk, mul))
+
+    for call in calls:
+        for kind, d, e in call:
+            b = R(d)
+            if b in gid:
+                continue
+            if kind == "far":
+                add([b], chunk_of[b], True)
+            elif kind == "p":
+                add([b], H, False)
+            else:
+                add(others, H, True)
+    add([rank], H, True)
 
     g.tensor.wait_ge(S.ld_f1, 16)
-    for k, (runs, _w, _a) in enumerate(groups):
-        p = T["p1_%d" % k]
-        g.tensor.wait_ge(S["ldx_%d" % k], 16 * len(runs))
-        for lo, hi in runs:
-            g.tensor.matmul(p[:, lo:hi], T.f1s[:], T.xs[:, lo:hi], True, True).then_inc(S["mm1_%d" % k], 1)
-        g.vector.wait_ge(S["ldt_%d" % k], 16 * len(runs))
-        g.vector.wait_ge(S["mm1_%d" % k], len(runs))
-        for lo, hi in runs:
-            g.vector.tensor_tensor(T.u[:, lo:hi], p[:, lo:hi], T.ts[:, lo:hi], AluOpType.mult).then_inc(S["u_%d" % k], 1)
+    for k, (lo, hi, c, mul) in enumerate(groups):
+        bank = T["b%d" % k]
+        g.tensor.wait_ge(S["ldx_%d" % c], nx[c])
+        g.tensor.matmul(bank[:, lo:hi], T.f1s[:], T.xs[:, lo:hi], True, True).then_inc(S["mm1_%d" % k], 1)
+        g.vector.wait_ge(S["mm1_%d" % k], 1)
+        if mul:
+            g.vector.wait_ge(S["ldt_%d" % c], nt[c])
+            g.vector.tensor_tensor(T.u[:, lo:hi], bank[:, lo:hi], T.ts[:, lo:hi], AluOpType.mult).then_inc(S["u_%d" % k], 1)
+        else:
+            g.vector.tensor_copy(T.u[:, lo:hi], bank[:, lo:hi]).then_inc(S["u_%d" % k], 1)
 
-    sent = 0
-    for k, (runs, writes, arr) in enumerate(groups):
-        if not writes:
-            continue
-        g.wait_ge(S["u_%d" % k], len(runs))
+    sent = len(pset)
+    rid, pid = topo.addr(nxt_c, core)
+    g.wait_ge(S.ld_tn, 16)
+    g.remote_dma_fused([RemoteDMATransfer(dst_ids=[DstId(rid=rid, pnc=pid)], dma_engine_mask=sum(pset),
+                                          remote_sem=S.arr_t, src=T.tn[:], dst=T.tl[:])], local_sem=S.sent)
+    for call in calls:
+        for k in sorted(set(gid[R(d)] for kind, d, e in call)):
+            g.wait_ge(S["u_%d" % k], 1)
         trs = []
-        for d, m, e in writes:
+        for kind, d, e in call:
             rid, pid = topo.addr(d, core)
-            r = T.rank_of(d)
-            trs.append(RemoteDMATransfer(dst_ids=[DstId(rid=rid, pnc=pid)], dma_engine_mask=m, remote_sem=arr,
+            r = R(d)
+            if kind == "far":
+                q = [i for i, grp in enumerate(_far_groups(topo, cores, d)) if core in grp][0]
+                arr = S["arr_far_%d" % q]
+            else:
+                arr = S.arr_p if kind == "p" else S.arr_near
+            trs.append(RemoteDMATransfer(dst_ids=[DstId(rid=rid, pnc=pid)], dma_engine_mask=sum(e), remote_sem=arr,
                                          src=T.u[:, r * w:(r + 1) * w], dst=T.land[:, own[0]:own[1]]))
-            sent += e
+            sent += len(e)
         g.remote_dma_fused(trs, local_sem=S.sent)
 
-    in_near = sum(e for j in near for d, m, e in _plan(topo, cores, cores[j])[1] if d == core)
-    got, cnt = [[], []], [0, 0]
-    for j in far:
-        for i, wv in enumerate(_plan(topo, cores, cores[j])[0]):
-            for d, m, e in wv:
-                if d == core:
-                    got[i].append(j)
-                    cnt[i] += e
-    pieces = [(i, lo, hi) for i in range(2) for lo, hi in _runs(got[i], w)]
+    in_t = len(_layout(topo, cores, prv_c)[5])
+    in_p = in_near = 0
+    near_from = []
+    for s in home_c:
+        if s == core:
+            continue
+        for call in _calls(topo, cores, s):
+            for kind, d, e in call:
+                if d == core and kind == "p":
+                    in_p += len(e)
+                if d == core and kind == "near":
+                    in_near += len(e)
+                    near_from.append(R(s))
+    near_runs = _runs(sorted(near_from), w)
+    pieces, cnt = [], []
+    for q, grp in enumerate(_far_groups(topo, cores, core)):
+        c = 0
+        for s in grp:
+            for call in _calls(topo, cores, s):
+                c += sum(len(e) for kind, d, e in call if d == core)
+        cnt.append(c)
+        for lo, hi in _runs(sorted(R(s) for s in grp), w):
+            pieces.append((q, lo, hi))
+    pv = (prv * w, (prv + 1) * w)
+    k_own = gid[rank]
 
     g.tensor.wait_ge(S.ld_f2, 16)
-    g.tensor.wait_ge(S["u_%d" % k_own], len(groups[k_own][0]))
-    g.tensor.matmul(T.p2own[:, own[0]:own[1]], T.f2s[:], T.u[:, own[0]:own[1]], True, True).then_inc(S.mm2_own, 1)
-    g.tensor.wait_ge(S.arr_near, in_near)
-    for lo, hi in near_runs:
-        g.tensor.matmul(T.p2near[:, lo:hi], T.f2s[:], T.land[:, lo:hi], True, True).then_inc(S.mm2_near, 1)
-    for q, (i, lo, hi) in enumerate(pieces):
-        g.tensor.wait_ge(S["arr_far_%d" % i], cnt[i])
-        g.tensor.matmul(T["p2far_%d" % q][:, lo:hi], T.f2s[:], T.land[:, lo:hi], True, True).then_inc(S["mm2_far_%d" % q], 1)
+    g.tensor.wait_ge(S["u_%d" % k_own], 1)
+    g.tensor.matmul(T.b6[:, own[0]:own[1]], T.f2s[:], T.u[:, own[0]:own[1]], True, True).then_inc(S.mm2_own, 1)
+    if near_runs:
+        g.tensor.wait_ge(S.arr_near, in_near)
+        for lo, hi in near_runs:
+            g.tensor.matmul(T.b7[:, lo:hi], T.f2s[:], T.land[:, lo:hi], True, True).then_inc(S.mm2_near, 1)
+    g.tensor.wait_ge(S.uq, 1)
+    g.tensor.wait_ge(S.u_0, 1)
+    g.tensor.matmul(T.b0[:, pv[0]:pv[1]], T.f2s[:], T.uq[:], True, True).then_inc(S.mm2_p, 1)
+    for i, (q, lo, hi) in enumerate(pieces):
+        g.tensor.wait_ge(S["arr_far_%d" % q], cnt[q])
+        g.tensor.wait_ge(S["u_%d" % (i + 1)], 1)
+        g.tensor.matmul(T["b%d" % (i + 1)][:, lo:hi], T.f2s[:], T.land[:, lo:hi], True, True).then_inc(S["mm2_far_%d" % i], 1)
 
     g.vector.wait_ge(S.mm2_own, 1)
-    g.vector.tensor_copy(T.ys[:, own[0]:own[1]], T.p2own[:, own[0]:own[1]]).then_inc(S.cp_own, 1)
-    g.vector.wait_ge(S.mm2_near, len(near_runs))
-    for lo, hi in near_runs:
-        g.vector.tensor_copy(T.ys[:, lo:hi], T.p2near[:, lo:hi]).then_inc(S.cp_near, 1)
-    for q, (i, lo, hi) in enumerate(pieces):
-        g.vector.wait_ge(S["mm2_far_%d" % q], 1)
-        g.vector.tensor_copy(T.ys[:, lo:hi], T["p2far_%d" % q][:, lo:hi]).then_inc(S["cp_far_%d" % q], 1)
+    g.vector.tensor_copy(T.ys[:, own[0]:own[1]], T.b6[:, own[0]:own[1]]).then_inc(S.cp_own, 1)
+    g.vector.wait_ge(S.arr_t, in_t)
+    g.vector.wait_ge(S.arr_p, in_p)
+    g.vector.tensor_tensor(T.uq[:], T.land[:, pv[0]:pv[1]], T.tl[:], AluOpType.mult).then_inc(S.uq, 1)
+    if near_runs:
+        g.vector.wait_ge(S.mm2_near, len(near_runs))
+        for lo, hi in near_runs:
+            g.vector.tensor_copy(T.ys[:, lo:hi], T.b7[:, lo:hi]).then_inc(S.cp_near, 1)
+    g.vector.wait_ge(S.mm2_p, 1)
+    g.vector.tensor_copy(T.ys[:, pv[0]:pv[1]], T.b0[:, pv[0]:pv[1]]).then_inc(S.cp_p, 1)
+    for i, (q, lo, hi) in enumerate(pieces):
+        g.vector.wait_ge(S["mm2_far_%d" % i], 1)
+        g.vector.tensor_copy(T.ys[:, lo:hi], T["b%d" % (i + 1)][:, lo:hi]).then_inc(S["cp_far_%d" % i], 1)
 
     g.sync.wait_ge(S.cp_own, 1)
-    g.sync.wait_ge(S.cp_near, len(near_runs))
+    if near_runs:
+        g.sync.wait_ge(S.cp_near, len(near_runs))
+    g.sync.wait_ge(S.cp_p, 1)
     for lo, hi in home_runs:
         g.sync.dma_start(T.y[:, lo:hi], T.ys[:, lo:hi]).then_inc(S.st_home, 16)
-    last = len(pieces) - 1
-    for q, (i, lo, hi) in enumerate(pieces):
-        eng = g.scalar if q == last else g.sync
-        eng.wait_ge(S["cp_far_%d" % q], 1)
-        eng.dma_start(T.y[:, lo:hi], T.ys[:, lo:hi]).then_inc(S["st_far_%d" % q], 16)
+    for i, (q, lo, hi) in enumerate(pieces):
+        g.scalar.wait_ge(S["cp_far_%d" % i], 1)
+        g.scalar.dma_start(T.y[:, lo:hi], T.ys[:, lo:hi]).then_inc(S["st_far_%d" % i], 16)
 
     g.wait_ge(S.sent, sent)
     g.sync.wait_ge(S.st_home, 16 * len(home_runs))
-    for q in range(len(pieces)):
-        (g.scalar if q == last else g.sync).wait_ge(S["st_far_%d" % q], 16)
+    for i in range(len(pieces)):
+        g.scalar.wait_ge(S["st_far_%d" % i], 16)

from concourse.bass import DstId, RemoteDMATransfer
from concourse.mybir import AluOpType

SCRATCH = {
    "f1s": ("sbuf", [128, 128], "bfloat16"),
    "f2s": ("sbuf", [128, 128], "bfloat16"),
    "xs": ("sbuf", [128, 384], "bfloat16"),
    "ts": ("sbuf", [128, 384], "bfloat16"),
    "tn": ("sbuf", [128, 64], "bfloat16"),
    "tl": ("sbuf", [128, 64], "bfloat16"),
    "uq": ("sbuf", [128, 64], "bfloat16"),
    "u": ("sbuf", [128, 384], "bfloat16"),
    "land": ("sbuf", [128, 384], "bfloat16"),
    "ys": ("sbuf", [128, 384], "bfloat16"),
}
for _k in range(8):
    SCRATCH["b%d" % _k] = ("psum", [128, 512], "float32")

SEMAPHORES = (["ld_tn", "ld_f1", "ld_f2", "arr_t", "arr_p", "arr_near", "sent", "uq",
               "mm2_own", "mm2_near", "mm2_p", "cp_own", "cp_near", "cp_p", "st_home"]
              + ["%s_%d" % (s, k) for s in ("arr_far", "mm2_far", "cp_far", "st_far") for k in range(2)]
              + ["%s_%d" % (s, k) for s in ("ldx", "ldt") for k in range(3)]
              + ["%s_%d" % (s, k) for s in ("mm1", "u") for k in range(6)])

ENG = 4


def _same_chip(topo, a, b):
    return topo.host(a) == topo.host(b) and topo.chip(a) == topo.chip(b)


def _bits(mask):
    return [1 << i for i in range(mask.bit_length()) if (mask >> i) & 1]


def _runs(blocks, w):
    out = []
    for b in blocks:
        if out and out[-1][1] == b * w:
            out[-1][1] = (b + 1) * w
        else:
            out.append([b * w, (b + 1) * w])
    return [(lo, hi) for lo, hi in out]


def _layout(topo, cores, src):
    home = [d for d in cores if _same_chip(topo, src, d)]
    far = [d for d in cores if not _same_chip(topo, src, d)]
    i = home.index(src)
    nxt = home[(i + 1) % len(home)]
    others = [d for d in home if d != src and d != nxt]
    rot = (i * len(far)) // len(home)
    far = far[rot:] + far[:rot]
    off = None
    for d in far:
        off = topo.mask(src, d) if off is None else off & topo.mask(src, d)
    on = None
    for d in home:
        if d != src:
            on = topo.mask(src, d) if on is None else on & topo.mask(src, d)
    off = _bits(off)
    sets = [off[0::2][:ENG], off[1::2][:ENG]]
    pset = [b for b in _bits(on) if b not in off][:ENG]
    return home, far, nxt, others, sets, pset


def _calls(topo, cores, src):
    home, far, nxt, others, sets, pset = _layout(topo, cores, src)
    calls = [[("far", d, sets[i % 2])] for i, d in enumerate(far)]
    nearc = [("p", nxt, pset)] + [("near", d, sets[i % 2]) for i, d in enumerate(others)]
    if others or len(calls) < 3:
        calls.append(nearc)
    else:
        calls[2] = calls[2] + nearc
    return calls


def _far_groups(topo, cores, dst):
    by = {}
    for s in cores:
        if not _same_chip(topo, s, dst):
            by.setdefault(_layout(topo, cores, s)[1].index(dst), []).append(s)
    return [by[k] for k in sorted(by)]


def rank_program(g, core, T, topo):
    rank = T.rank_of(core)
    if rank is None:
        return
    cores = list(T.cores)
    n = len(cores)
    w = T.x.shape[1] // n
    S = T.sem
    R = T.rank_of
    home_c, far_c, nxt_c, others_c, sets, pset = _layout(topo, cores, core)
    home = sorted(R(d) for d in home_c)
    nxt = R(nxt_c)
    others = sorted(R(d) for d in others_c)
    prv_c = [d for d in home_c if d != core and _layout(topo, cores, d)[2] == core][0]
    prv = R(prv_c)
    home_runs = _runs(home, w)
    own = (rank * w, (rank + 1) * w)
    calls = _calls(topo, cores, core)

    far_r = [R(d) for d in far_c]
    chunks = [far_r[i:i + 2] for i in range(0, len(far_r), 2)]
    H = len(chunks)
    chunk_of = {}
    for c, bl in enumerate(chunks):
        for b in bl:
            chunk_of[b] = c
    t_home = _runs(sorted(others + [rank]), w)
    if len(t_home) > len(home_runs):
        t_home = home_runs

    loads = [(T.tn[:], T.t[:, nxt * w:(nxt + 1) * w], S.ld_tn), (T.f1s[:], T.f1[:], S.ld_f1)]
    nx, nt = {}, {}
    for c, bl in enumerate(chunks):
        rr = _runs(sorted(bl), w)
        nx[c] = nt[c] = 16 * len(rr)
        for lo, hi in rr:
            loads.append((T.xs[:, lo:hi], T.x[:, lo:hi], S["ldx_%d" % c]))
            loads.append((T.ts[:, lo:hi], T.t[:, lo:hi], S["ldt_%d" % c]))
    nx[H], nt[H] = 16 * len(home_runs), 16 * len(t_home)
    for lo, hi in home_runs:
        loads.append((T.xs[:, lo:hi], T.x[:, lo:hi], S["ldx_%d" % H]))
    for lo, hi in t_home:
        loads.append((T.ts[:, lo:hi], T.t[:, lo:hi], S["ldt_%d" % H]))
    loads.append((T.f2s[:], T.f2[:], S.ld_f2))
    for i, (o, a, s) in enumerate(loads):
        (g.sync if i % 2 == 0 else g.scalar).dma_start(o, a).then_inc(s, 16)

    groups, gid = [], {}

    def add(blocks, chunk, mul):
        for lo, hi in _runs(sorted(blocks), w):
            for b in blocks:
                if lo <= b * w < hi:
                    gid[b] = len(groups)
            groups.append((lo, hi, chunk, mul))

    for call in calls:
        for kind, d, e in call:
            b = R(d)
            if b in gid:
                continue
            if kind == "far":
                add([b], chunk_of[b], True)
            elif kind == "p":
                add([b], H, False)
            else:
                add(others, H, True)
    add([rank], H, True)

    g.tensor.wait_ge(S.ld_f1, 16)
    for k, (lo, hi, c, mul) in enumerate(groups):
        bank = T["b%d" % k]
        g.tensor.wait_ge(S["ldx_%d" % c], nx[c])
        g.tensor.matmul(bank[:, lo:hi], T.f1s[:], T.xs[:, lo:hi], True, True).then_inc(S["mm1_%d" % k], 1)
        g.vector.wait_ge(S["mm1_%d" % k], 1)
        if mul:
            g.vector.wait_ge(S["ldt_%d" % c], nt[c])
            g.vector.tensor_tensor(T.u[:, lo:hi], bank[:, lo:hi], T.ts[:, lo:hi], AluOpType.mult).then_inc(S["u_%d" % k], 1)
        else:
            g.vector.tensor_copy(T.u[:, lo:hi], bank[:, lo:hi]).then_inc(S["u_%d" % k], 1)

    sent = len(pset)
    rid, pid = topo.addr(nxt_c, core)
    g.wait_ge(S.ld_tn, 16)
    g.remote_dma_fused([RemoteDMATransfer(dst_ids=[DstId(rid=rid, pnc=pid)], dma_engine_mask=sum(pset),
                                          remote_sem=S.arr_t, src=T.tn[:], dst=T.tl[:])], local_sem=S.sent)
    for call in calls:
        for k in sorted(set(gid[R(d)] for kind, d, e in call)):
            g.wait_ge(S["u_%d" % k], 1)
        trs = []
        for kind, d, e in call:
            rid, pid = topo.addr(d, core)
            r = R(d)
            if kind == "far":
                q = [i for i, grp in enumerate(_far_groups(topo, cores, d)) if core in grp][0]
                arr = S["arr_far_%d" % q]
            else:
                arr = S.arr_p if kind == "p" else S.arr_near
            trs.append(RemoteDMATransfer(dst_ids=[DstId(rid=rid, pnc=pid)], dma_engine_mask=sum(e), remote_sem=arr,
                                         src=T.u[:, r * w:(r + 1) * w], dst=T.land[:, own[0]:own[1]]))
            sent += len(e)
        g.remote_dma_fused(trs, local_sem=S.sent)

    in_t = len(_layout(topo, cores, prv_c)[5])
    in_p = in_near = 0
    near_from = []
    for s in home_c:
        if s == core:
            continue
        for call in _calls(topo, cores, s):
            for kind, d, e in call:
                if d == core and kind == "p":
                    in_p += len(e)
                if d == core and kind == "near":
                    in_near += len(e)
                    near_from.append(R(s))
    near_runs = _runs(sorted(near_from), w)
    pieces, cnt = [], []
    for q, grp in enumerate(_far_groups(topo, cores, core)):
        c = 0
        for s in grp:
            for call in _calls(topo, cores, s):
                c += sum(len(e) for kind, d, e in call if d == core)
        cnt.append(c)
        for lo, hi in _runs(sorted(R(s) for s in grp), w):
            pieces.append((q, lo, hi))
    pv = (prv * w, (prv + 1) * w)
    k_own = gid[rank]

    g.tensor.wait_ge(S.ld_f2, 16)
    g.tensor.wait_ge(S["u_%d" % k_own], 1)
    g.tensor.matmul(T.b6[:, own[0]:own[1]], T.f2s[:], T.u[:, own[0]:own[1]], True, True).then_inc(S.mm2_own, 1)
    if near_runs:
        g.tensor.wait_ge(S.arr_near, in_near)
        for lo, hi in near_runs:
            g.tensor.matmul(T.b7[:, lo:hi], T.f2s[:], T.land[:, lo:hi], True, True).then_inc(S.mm2_near, 1)
    g.tensor.wait_ge(S.uq, 1)
    g.tensor.wait_ge(S.u_0, 1)
    g.tensor.matmul(T.b0[:, pv[0]:pv[1]], T.f2s[:], T.uq[:], True, True).then_inc(S.mm2_p, 1)
    for i, (q, lo, hi) in enumerate(pieces):
        g.tensor.wait_ge(S["arr_far_%d" % q], cnt[q])
        g.tensor.wait_ge(S["u_%d" % (i + 1)], 1)
        g.tensor.matmul(T["b%d" % (i + 1)][:, lo:hi], T.f2s[:], T.land[:, lo:hi], True, True).then_inc(S["mm2_far_%d" % i], 1)

    g.vector.wait_ge(S.mm2_own, 1)
    g.vector.tensor_copy(T.ys[:, own[0]:own[1]], T.b6[:, own[0]:own[1]]).then_inc(S.cp_own, 1)
    g.vector.wait_ge(S.arr_t, in_t)
    g.vector.wait_ge(S.arr_p, in_p)
    g.vector.tensor_tensor(T.uq[:], T.land[:, pv[0]:pv[1]], T.tl[:], AluOpType.mult).then_inc(S.uq, 1)
    if near_runs:
        g.vector.wait_ge(S.mm2_near, len(near_runs))
        for lo, hi in near_runs:
            g.vector.tensor_copy(T.ys[:, lo:hi], T.b7[:, lo:hi]).then_inc(S.cp_near, 1)
    g.vector.wait_ge(S.mm2_p, 1)
    g.vector.tensor_copy(T.ys[:, pv[0]:pv[1]], T.b0[:, pv[0]:pv[1]]).then_inc(S.cp_p, 1)
    for i, (q, lo, hi) in enumerate(pieces):
        g.vector.wait_ge(S["mm2_far_%d" % i], 1)
        g.vector.tensor_copy(T.ys[:, lo:hi], T["b%d" % (i + 1)][:, lo:hi]).then_inc(S["cp_far_%d" % i], 1)

    g.sync.wait_ge(S.cp_own, 1)
    if near_runs:
        g.sync.wait_ge(S.cp_near, len(near_runs))
    g.sync.wait_ge(S.cp_p, 1)
    for lo, hi in home_runs:
        g.sync.dma_start(T.y[:, lo:hi], T.ys[:, lo:hi]).then_inc(S.st_home, 16)
    for i, (q, lo, hi) in enumerate(pieces):
        g.scalar.wait_ge(S["cp_far_%d" % i], 1)
        g.scalar.dma_start(T.y[:, lo:hi], T.ys[:, lo:hi]).then_inc(S["st_far_%d" % i], 16)

    g.wait_ge(S.sent, sent)
    g.sync.wait_ge(S.st_home, 16 * len(home_runs))
    for i in range(len(pieces)):
        g.scalar.wait_ge(S["st_far_%d" % i], 16)
